import numpy as np
import ml_dtypes


def mxq(x, axis, fmt="e4m3"):
    dtype, down = {"e4m3": (ml_dtypes.float8_e4m3fn, 7), "e5m2": (ml_dtypes.float8_e5m2, 14)}[fmt]
    v = np.moveaxis(np.asarray(x, np.float32).astype(ml_dtypes.bfloat16).astype(np.float64), axis, -1)
    blocks = v.reshape(v.shape[:-1] + (-1, 32))
    amax = np.abs(blocks).max(-1, keepdims=True)
    byte = np.maximum(np.where(amax > 0, np.frexp(amax)[1] - 1 + 127, 0) - down, 1)
    scale = np.exp2(byte - 127.0)
    codes = (blocks / scale).astype(np.float32).astype(dtype).astype(np.float64)
    return np.moveaxis((codes * scale).reshape(v.shape), -1, axis)


WIDE = False


def mx_kscale(k):
    if not WIDE:
        return np.ones(k)
    levels = np.array([10, -10, 5, -5, 0])
    if k % 512:
        return np.exp2(np.random.permutation(np.resize(levels, k // 32))).repeat(32)
    a = np.empty((k // 512, 16))
    for p in range(k // 512):
        a[p, :8] = np.random.permutation(np.resize(levels, 8))
        for g in range(8):
            far = levels[np.abs(levels - a[p, g]) >= 10]
            a[p, g + 8] = far[np.random.randint(len(far))]
    return np.exp2(a.ravel()).repeat(32)


def f64(x):
    return np.asarray(x).astype(np.float64)


def striped(idx):
    return np.tile(np.asarray(idx).reshape(-1, 16).T, (8, 1)).astype(np.uint16)


def unstriped(offs):
    return offs[:16].T.reshape(-1).astype(np.int64)


E2M1 = np.array([0.0, 0.5, 1.0, 1.5, 2.0, 3.0, 4.0, 6.0, -0.0, -0.5, -1.0, -1.5, -2.0, -3.0, -4.0, -6.0])


def pack_weight(w, fmt):
    k, n = w.shape
    w = f64(np.asarray(w, np.float32).astype(ml_dtypes.bfloat16)).reshape(k // 32, 32, n)
    amax = np.abs(w).max(1)
    if fmt == "e4m3":
        byte = np.frexp(amax)[1] - 1 + 127 - 7
    else:
        mant, ex = np.frexp(amax / 6.0)
        byte = np.where(mant > 0.5, ex, ex - 1) + 127
    byte = np.clip(np.where(amax > 0, byte, 1), 1, 254)
    scaled = (w * np.exp2(127.0 - byte)[:, None, :]).reshape(k, n).astype(np.float32)
    by_word = np.ascontiguousarray(scaled.reshape(k // 512, 128, 4, n).transpose(0, 1, 3, 2))
    if fmt == "e4m3":
        words = by_word.astype(ml_dtypes.float8_e4m3fn).view(np.uint8)
    else:
        c = by_word.astype(ml_dtypes.float4_e2m1fn).view(np.uint8) & 0xF
        words = (c[..., 0::2] | (c[..., 1::2] << 4)).reshape(k // 512, 128, 2 * n)
    return np.ascontiguousarray(words), np.ascontiguousarray(byte.astype(np.uint8).reshape(k // 512, 16, n))


def unpack_weight(words, scales, fmt):
    g, _, n = scales.shape
    words = np.ascontiguousarray(words).reshape(g, 128, n, -1)
    if fmt == "e4m3":
        vals = words.view(ml_dtypes.float8_e4m3fn).astype(np.float64)
    else:
        nib = np.empty((g, 128, n, 4), np.uint8)
        nib[..., 0::2] = words & 0xF
        nib[..., 1::2] = words >> 4
        vals = E2M1[nib]
    vals = vals * np.repeat(np.exp2(scales.astype(np.float64) - 127.0), 8, axis=1)[..., None]
    return vals.transpose(0, 1, 3, 2).reshape(g * 512, n)


D, T, I, Q, E, K = 512, 2048, 512, 256, 512, 512


def setup_inputs():
    n = np.random.standard_normal
    idx = np.random.permutation(T)[:I]
    fd = mx_kscale(D)
    fi = mx_kscale(I)
    fk = mx_kscale(K)
    ti = np.ones(T)
    ti[idx] = fi
    keysp = pack_weight(n((D, T)) / fd[:, None], "e2m1")
    return {
        "query": (n((D, Q)) * 0.25 / np.sqrt(D) * fd[:, None]).astype(np.float32),
        "keys_words": keysp[0],
        "keys_scales": keysp[1],
        "size": (np.random.uniform(4.0, 12.0, (1, I)) * fi).astype(np.float32),
        "vals": (n((E, T)) / ti).astype(np.float32),
        "cond": (n((K, Q)) * fk[:, None]).astype(np.float32),
        "wg": (n((K, E)) * 0.5 / np.sqrt(K) / fk[:, None]).astype(np.float32),
        "wb": (n((K, E)) * 0.3 / np.sqrt(K) / fk[:, None]).astype(np.float32),
        "offs": striped(idx),
    }


def reference(query, keys_words, keys_scales, size, vals, cond, wg, wb, offs):
    idx = unstriped(offs)
    keysu = unpack_weight(keys_words, keys_scales, "e2m1")
    queryq = mxq(f64(query), 0, "e4m3")
    keysidxg = keysu[:, idx]
    a = queryq.T @ keysidxg
    p = np.exp(a - np.max(a, axis=1, keepdims=True))
    w = p * f64(size) / np.sum(p, axis=1, keepdims=True)
    wt = w.T
    vt = f64(vals)[:, idx].T
    vtq = mxq(vt, 0, "e4m3")
    wtq = mxq(wt, 0, "e4m3")
    o = vtq.T @ wtq
    wgq = mxq(f64(wg), 0, "e4m3")
    condq = mxq(f64(cond), 0, "e4m3")
    g = wgq.T @ condq
    wbq = mxq(f64(wb), 0, "e4m3")
    b = wbq.T @ condq
    y = o * (1.0 + g) + b
    return y

@@ -1,0 +1,243 @@
+from contextlib import ExitStack
+
+import concourse.mybir as mybir
+from concourse.masks import make_identity
+
+D, T, I, Q, E, K = 512, 2048, 512, 256, 512, 512
+FLOPS = 2 * Q * I * D + 2 * E * Q * I + 2 * 2 * E * Q * K
+
+F32 = mybir.dt.float32
+BF16 = mybir.dt.bfloat16
+I32 = mybir.dt.int32
+U32 = mybir.dt.uint32
+U16 = mybir.dt.uint16
+U8 = mybir.dt.uint8
+FP8X4 = mybir.dt.float8_e4m3fn_x4
+FP4X4 = mybir.dt.float4_e2m1fn_x4
+ALU = mybir.AluOpType
+ACT = mybir.ActivationFunctionType
+AX = mybir.AxisListType
+
+P = 128
+PACK = 4
+HALF = 256
+
+
+def tile_attend_filmattn_kernel(tc, query, keys_words, keys_scales, size, vals, cond, wg, wb, offs, out):
+    nc = tc.nc
+    with ExitStack() as ctx:
+        sb = ctx.enter_context(tc.tile_pool(name="sb", bufs=1))
+        ps = ctx.enter_context(tc.psum_pool(name="ps", bufs=1))
+
+        def bank(n, name):
+            return ps.tile([P, 512], F32, tag="bank%d" % n, name=name)
+
+        def load_rows(name, src):
+            raw = sb.tile([P, PACK, HALF], F32, name=name + "_raw")
+            nc.sync.dma_start(out=raw[:], in_=src)
+            return raw
+
+        def weave(copy, name, raw):
+            woven = sb.tile([P, raw.shape[2], PACK], BF16, name=name + "_bf", tag=name + "_bf", align_bytes=64)
+            copy(
+                out=woven[:].rearrange("p (c i) t -> p c t i", i=4),
+                in_=raw.rearrange("p t (c i) -> p c t i", i=4),
+            )
+            return woven
+
+        def quantise(name, woven, slot=None):
+            width = woven.shape[1]
+            codes = sb.tile([P, width], U32, name=name + "_codes", tag=slot or name + "_codes", align_bytes=64)
+            scales = sb.tile([P, width], U8, name=name + "_scales", align_bytes=64)
+            nc.vector.quantize_mx(
+                out=codes[:].bitcast(FP8X4), scales=scales[:], in_=woven[:].rearrange("p c t -> p (c t)")
+            )
+            return codes, scales
+
+        def product(dst, stat, cols, mov):
+            nc.tensor.matmul_mx(
+                out=dst,
+                lhsT=stat[0][:, cols].bitcast(FP8X4),
+                lhsT_scale=stat[1][:, cols],
+                rhs=mov[0][:].bitcast(FP8X4),
+                rhs_scale=mov[1][:],
+                start=True,
+                stop=True,
+            )
+
+        def turn(dst, src_bf):
+            words = src_bf[:].bitcast(F32)
+            for u in range(2):
+                nc.tensor.transpose(dst[:, P * u : P * (u + 1)], words[:, u : 2 * P : 2], ident[:])
+
+        def load_vals(j):
+            pool_j = sb.tile([P, T], F32, name="val_pool%d" % j, tag="val_pool%d" % j, align_bytes=64)
+            nc.sync.dma_start(out=pool_j[:], in_=vals[P * j : P * (j + 1), :])
+            return pool_j
+
+        def rows4(ap):
+            return ap.rearrange("(p j) c -> p j c", j=PACK)
+
+        def load_half(name, w, h):
+            return load_rows("%s%d" % (name, h), rows4(w)[:, :, HALF * h : HALF * (h + 1)])
+
+        def cols(c):
+            return slice(P * c, P * (c + 1))
+
+        scale_pool = sb.tile([P, T], U8, name="scale_pool", align_bytes=64)
+        nc.gpsimd.memset(scale_pool[:].bitcast(I32), 0)
+        offsets = sb.tile([P, I // 16], U16, name="offsets")
+        nc.sync.dma_start(offsets[:], offs)
+        size_col = sb.tile([P, PACK], F32, name="size_col")
+        nc.sync.dma_start(out=size_col[:], in_=size.rearrange("o (p t) -> p (o t)", t=PACK))
+        key_pool = sb.tile([P, T], U16, name="key_pool", align_bytes=64)
+        nc.sync.dma_start(out=key_pool[:].bitcast(I32), in_=keys_words[0].bitcast(I32))
+        for quad in range(4):
+            nc.sync.dma_start(
+                out=scale_pool[32 * quad : 32 * quad + 4, :].bitcast(I32),
+                in_=keys_scales[0, 4 * quad : 4 * quad + 4, :].bitcast(I32),
+            )
+        query_raw = load_rows("query", rows4(query))
+        cond_raw = load_rows("cond", rows4(cond))
+        val_pool = [load_vals(0)]
+        wg_raw = [load_half("wg", wg, 0)]
+        val_pool.append(load_vals(1))
+        wg_raw.append(load_half("wg", wg, 1))
+        val_pool.extend([load_vals(2), load_vals(3)])
+        wb_raw = [load_half("wb", wb, h) for h in range(2)]
+
+        ident = sb.tile([P, P], F32, name="ident")
+        make_identity(nc, ident[:])
+
+        key_codes = sb.tile([P, I], U16, name="key_codes", align_bytes=64)
+        nc.vector.tensor_copy(key_codes[:], key_pool[:].indirect(offsets[:]))
+        key_scales = sb.tile([P, I], U8, name="key_scales", align_bytes=64)
+        nc.vector.tensor_copy(key_scales[:], scale_pool[:].indirect(offsets[:]))
+
+        scores = []
+        for h in range(2):
+            query_q = quantise("query%d" % h, weave(nc.scalar.copy, "query%d" % h, query_raw[:, :, cols(h)]))
+            score = bank(h, "score%d" % h)
+            nc.tensor.matmul_mx(
+                out=score[:],
+                lhsT=query_q[0][:].bitcast(FP8X4),
+                lhsT_scale=query_q[1][:],
+                rhs=key_codes[:].bitcast(FP4X4),
+                rhs_scale=key_scales[:],
+                start=True,
+                stop=True,
+            )
+            scores.append(score)
+
+        cond_bf = weave(nc.scalar.copy, "cond", cond_raw[:])
+        size_rows = bank(2, "size_rows")
+        for t in range(PACK):
+            nc.tensor.transpose(size_rows[:, cols(t)], size_col[:, t : t + 1].to_broadcast([P, P]), ident[:])
+
+        probs, sums = [], []
+        for h in range(2):
+            neg_max = sb.tile([P, 1], F32, name="neg_max%d" % h)
+            nc.vector.tensor_reduce(out=neg_max[:], in_=scores[h][:], axis=AX.X, op=ALU.max, negate=True)
+            prob = sb.tile([P, I], F32, name="prob%d" % h, tag="prob%d" % h, align_bytes=64)
+            row_sum = sb.tile([P, 1], F32, name="row_sum%d" % h, tag="row_sum%d" % h, align_bytes=64)
+            nc.scalar.activation(out=prob[:], in_=scores[h][:], func=ACT.Exp, bias=neg_max[:], accum_out=row_sum[:])
+            probs.append(prob)
+            sums.append(row_sum)
+
+        def gather_vals(j):
+            picked = sb.tile([P, I], BF16, name="picked%d" % j, align_bytes=64)
+            nc.vector.tensor_copy(picked[:], val_pool[j][:].indirect(offsets[:]))
+            turned = bank(4 + j % 2, "val_turned%d" % j)
+            turn(turned[:, 0:HALF], picked)
+            woven = sb.tile([P, P, PACK], BF16, name="val_bf%d" % j, align_bytes=64)
+            nc.scalar.copy(out=woven[:].bitcast(F32), in_=turned[:, 0:HALF].rearrange("p (u e) -> p e u", u=2))
+            return woven
+
+        def attend(j, val_q):
+            attn = bank(j % 2, "attn%d" % j)
+            product(attn[:, 0:Q], val_q, cols(0), weight_q)
+            return attn
+
+        def make_gain(h, wg_q):
+            gain_ps = bank((7, 2)[h], "gain_ps%d" % h)
+            for c in range(2):
+                product(gain_ps[:, Q * c : Q * (c + 1)], wg_q, cols(c), cond_q)
+            gain = sb.tile([P, 2 * Q], F32, name="gain%d" % h)
+            nc.scalar.copy(out=gain[:], in_=gain_ps[:])
+            return gain
+
+        def modulate(j, part, attn, gain):
+            nc.vector.scalar_tensor_tensor(
+                out=part,
+                in0=gain[:, Q * (j % 2) : Q * (j % 2 + 1)],
+                scalar=1.0,
+                in1=attn[:, 0:Q],
+                op0=ALU.add,
+                op1=ALU.mult,
+            )
+
+        def make_shift(j, wb_q, c):
+            shift = bank((3, 6, 2, 7)[j], "shift%d" % j)
+            product(shift[:, 0:Q], wb_q, cols(c), cond_q)
+            return shift
+
+        def finish(j, shift, part):
+            result = sb.tile([P, Q], F32, name="result%d" % j)
+            nc.vector.tensor_tensor(out=result[:], in0=shift[:, 0:Q], in1=part, op=ALU.add)
+            nc.sync.dma_start(out=out[cols(j), :], in_=result[:])
+
+        cond_q = quantise("cond", cond_bf)
+        val_bf = [gather_vals(0)]
+        wg_bf = weave(nc.scalar.copy, "wg0", wg_raw[0][:])
+
+        weight_bf = sb.tile([P, Q, PACK], BF16, name="weight_bf", align_bytes=64)
+        for h in range(2):
+            inv_sum = sb.tile([P, 1], F32, name="inv_sum%d" % h, tag=("val_pool0", "inv_sum1")[h], align_bytes=64)
+            nc.vector.reciprocal(out=inv_sum[:], in_=sums[h][:])
+            weight = sb.tile([P, I], BF16, name="weight%d" % h, align_bytes=64)
+            nc.vector.scalar_tensor_tensor(
+                out=weight[:].rearrange("q (s t) -> q s t", t=PACK),
+                in0=probs[h][:].rearrange("q (s t) -> q s t", t=PACK),
+                scalar=inv_sum[:],
+                in1=size_rows[:].rearrange("q (t s) -> q s t", t=PACK),
+                op0=ALU.mult,
+                op1=ALU.mult,
+            )
+            weight_turned = bank((3, 6)[h], "weight_turned%d" % h)
+            turn(weight_turned[:, 0:HALF], weight)
+            nc.scalar.copy(
+                out=weight_bf[:, cols(h), :].bitcast(F32),
+                in_=weight_turned[:, 0:HALF].rearrange("p (u q) -> p q u", u=2),
+            )
+        val_bf.append(gather_vals(1))
+        val_q = [quantise("val0", val_bf[0], slot="inv_sum1")]
+        gains = [make_gain(0, quantise("wg0", wg_bf, slot="prob1"))]
+        gains.append(make_gain(1, quantise("wg1", weave(nc.vector.tensor_copy, "wg1", wg_raw[1][:]))))
+        weight_q = quantise("weight", weight_bf, slot="wg1_bf")
+        val_q.append(quantise("val1", val_bf[1]))
+        attn = [attend(j, val_q[j]) for j in range(2)]
+
+        val_bf.append(gather_vals(2))
+        early = sb.tile([P, 2, Q], F32, name="early", tag="val_pool2", align_bytes=64)
+        parts = [early[:, 0, :], early[:, 1, :]]
+        for j in range(2):
+            modulate(j, parts[j], attn[j], gains[0])
+        val_bf.append(gather_vals(3))
+        attn.append(attend(2, quantise("val2", val_bf[2], slot="val_pool3")))
+        wb_bf = [
+            weave(nc.scalar.copy, "wb0", wb_raw[0][:]),
+            weave(nc.vector.tensor_copy, "wb2", wb_raw[1][:, :, cols(0)]),
+            weave(nc.scalar.copy, "wb3", wb_raw[1][:, :, cols(1)]),
+        ]
+        wb_q = [quantise("wb0", wb_bf[0])]
+        part2 = sb.tile([P, Q], F32, name="part2")
+        modulate(2, part2[:], attn[2], gains[1])
+        wb_q.append(quantise("wb2", wb_bf[1]))
+        attn.append(attend(3, quantise("val3", val_bf[3], slot="wb2_bf")))
+        for j in range(2):
+            finish(j, make_shift(j, wb_q[0], j), parts[j])
+        wb_q.append(quantise("wb3", wb_bf[2]))
+        finish(2, make_shift(2, wb_q[1], 0), part2[:])
+        part3 = sb.tile([P, Q], F32, name="part3", tag="val_pool2", align_bytes=64)
+        modulate(3, part3[:], attn[3], gains[1])
+        finish(3, make_shift(3, wb_q[2], 0), part3[:])

@@ -32,35 +32,39 @@ def tile_attend_filmattn_kernel(tc, query, keys_words, keys_scales, size, vals, 
         def bank(n, name):
             return ps.tile([P, 512], F32, tag="bank%d" % n, name=name)
 
+        def held(shape, dtype, name, slot=None):
+            return sb.tile(shape, dtype, name=name, tag=slot or name, align_bytes=64)
+
         def load_rows(name, src):
-            raw = sb.tile([P, PACK, HALF], F32, name=name + "_raw")
+            raw = held([P, PACK, HALF], F32, name + "_raw")
             nc.sync.dma_start(out=raw[:], in_=src)
             return raw
 
-        def weave(copy, name, raw):
-            woven = sb.tile([P, raw.shape[2], PACK], BF16, name=name + "_bf", tag=name + "_bf", align_bytes=64)
+        def weave(copy, woven, raw):
             copy(
-                out=woven[:].rearrange("p (c i) t -> p c t i", i=4),
+                out=woven.rearrange("p (c i) t -> p c t i", i=4),
                 in_=raw.rearrange("p t (c i) -> p c t i", i=4),
             )
-            return woven
 
         def quantise(name, woven, slot=None):
             width = woven.shape[1]
-            codes = sb.tile([P, width], U32, name=name + "_codes", tag=slot or name + "_codes", align_bytes=64)
-            scales = sb.tile([P, width], U8, name=name + "_scales", align_bytes=64)
+            codes = held([P, width], U32, name + "_codes", slot)
+            scales = held([P, width], U8, name + "_scales")
             nc.vector.quantize_mx(
                 out=codes[:].bitcast(FP8X4), scales=scales[:], in_=woven[:].rearrange("p c t -> p (c t)")
             )
-            return codes, scales
+            return codes[:], scales[:]
+
+        def window(quantised, first, width):
+            return quantised[0][:, first : first + width], quantised[1][:, first : first + width]
 
         def product(dst, stat, cols, mov):
             nc.tensor.matmul_mx(
                 out=dst,
                 lhsT=stat[0][:, cols].bitcast(FP8X4),
                 lhsT_scale=stat[1][:, cols],
-                rhs=mov[0][:].bitcast(FP8X4),
-                rhs_scale=mov[1][:],
+                rhs=mov[0].bitcast(FP8X4),
+                rhs_scale=mov[1],
                 start=True,
                 stop=True,
             )
@@ -84,13 +88,14 @@ def tile_attend_filmattn_kernel(tc, query, keys_words, keys_scales, size, vals, 
         def cols(c):
             return slice(P * c, P * (c + 1))
 
-        scale_pool = sb.tile([P, T], U8, name="scale_pool", align_bytes=64)
+        scale_pool = held([P, T], U8, "scale_pool")
         nc.gpsimd.memset(scale_pool[:].bitcast(I32), 0)
         offsets = sb.tile([P, I // 16], U16, name="offsets")
         nc.sync.dma_start(offsets[:], offs)
+        val_pool, wg_raw, wb_raw = {}, {}, {}
         size_col = sb.tile([P, PACK], F32, name="size_col")
         nc.sync.dma_start(out=size_col[:], in_=size.rearrange("o (p t) -> p (o t)", t=PACK))
-        key_pool = sb.tile([P, T], U16, name="key_pool", align_bytes=64)
+        key_pool = held([P, T], U16, "key_pool")
         nc.sync.dma_start(out=key_pool[:].bitcast(I32), in_=keys_words[0].bitcast(I32))
         for quad in range(4):
             nc.sync.dma_start(
@@ -99,106 +104,60 @@ def tile_attend_filmattn_kernel(tc, query, keys_words, keys_scales, size, vals, 
             )
         query_raw = load_rows("query", rows4(query))
         cond_raw = load_rows("cond", rows4(cond))
-        val_pool = [load_vals(0)]
-        wg_raw = [load_half("wg", wg, 0)]
-        val_pool.append(load_vals(1))
-        wg_raw.append(load_half("wg", wg, 1))
-        val_pool.extend([load_vals(2), load_vals(3)])
-        wb_raw = [load_half("wb", wb, h) for h in range(2)]
+        wg_raw[0] = load_half("wg", wg, 0)
+        val_pool[0] = load_vals(0)
+        wg_raw[1] = load_half("wg", wg, 1)
+        val_pool[1] = load_vals(1)
+        val_pool[2] = load_vals(2)
+        val_pool[3] = load_vals(3)
+        wb_raw[0] = load_half("wb", wb, 0)
+        wb_raw[1] = load_half("wb", wb, 1)
 
         ident = sb.tile([P, P], F32, name="ident")
         make_identity(nc, ident[:])
 
-        key_codes = sb.tile([P, I], U16, name="key_codes", align_bytes=64)
+        key_codes = held([P, I], U16, "key_codes")
         nc.vector.tensor_copy(key_codes[:], key_pool[:].indirect(offsets[:]))
-        key_scales = sb.tile([P, I], U8, name="key_scales", align_bytes=64)
+        key_scales = held([P, I], U8, "key_scales")
         nc.vector.tensor_copy(key_scales[:], scale_pool[:].indirect(offsets[:]))
 
-        scores = []
-        for h in range(2):
-            query_q = quantise("query%d" % h, weave(nc.scalar.copy, "query%d" % h, query_raw[:, :, cols(h)]))
-            score = bank(h, "score%d" % h)
+        size_rows = bank(2, "size_rows")
+        for t in range(PACK):
+            nc.tensor.transpose(size_rows[:, cols(t)], size_col[:, t : t + 1].to_broadcast([P, P]), ident[:])
+
+        query_bf = [held([P, P, PACK], BF16, "query_bf%d" % h) for h in range(2)]
+        gains = held([P, 4 * Q], F32, "gains")
+        scores, probs = {}, {}
+        prob_pair = held([P, 2, I], F32, "prob_pair", "wg0_raw")
+        row_sums = held([P, 2], F32, "row_sums")
+
+        def score(h):
+            query_q = quantise("query%d" % h, query_bf[h])
+            scores[h] = bank(h, "score%d" % h)
             nc.tensor.matmul_mx(
-                out=score[:],
-                lhsT=query_q[0][:].bitcast(FP8X4),
-                lhsT_scale=query_q[1][:],
+                out=scores[h][:],
+                lhsT=query_q[0].bitcast(FP8X4),
+                lhsT_scale=query_q[1],
                 rhs=key_codes[:].bitcast(FP4X4),
                 rhs_scale=key_scales[:],
                 start=True,
                 stop=True,
             )
-            scores.append(score)
 
-        cond_bf = weave(nc.scalar.copy, "cond", cond_raw[:])
-        size_rows = bank(2, "size_rows")
-        for t in range(PACK):
-            nc.tensor.transpose(size_rows[:, cols(t)], size_col[:, t : t + 1].to_broadcast([P, P]), ident[:])
-
-        probs, sums = [], []
-        for h in range(2):
-            neg_max = sb.tile([P, 1], F32, name="neg_max%d" % h)
+        def soften(h):
+            neg_max = held([P, 1], F32, "neg_max%d" % h, ("neg_max0", "neg_max1")[h])
             nc.vector.tensor_reduce(out=neg_max[:], in_=scores[h][:], axis=AX.X, op=ALU.max, negate=True)
-            prob = sb.tile([P, I], F32, name="prob%d" % h, tag="prob%d" % h, align_bytes=64)
-            row_sum = sb.tile([P, 1], F32, name="row_sum%d" % h, tag="row_sum%d" % h, align_bytes=64)
-            nc.scalar.activation(out=prob[:], in_=scores[h][:], func=ACT.Exp, bias=neg_max[:], accum_out=row_sum[:])
-            probs.append(prob)
-            sums.append(row_sum)
-
-        def gather_vals(j):
-            picked = sb.tile([P, I], BF16, name="picked%d" % j, align_bytes=64)
-            nc.vector.tensor_copy(picked[:], val_pool[j][:].indirect(offsets[:]))
-            turned = bank(4 + j % 2, "val_turned%d" % j)
-            turn(turned[:, 0:HALF], picked)
-            woven = sb.tile([P, P, PACK], BF16, name="val_bf%d" % j, align_bytes=64)
-            nc.scalar.copy(out=woven[:].bitcast(F32), in_=turned[:, 0:HALF].rearrange("p (u e) -> p e u", u=2))
-            return woven
-
-        def attend(j, val_q):
-            attn = bank(j % 2, "attn%d" % j)
-            product(attn[:, 0:Q], val_q, cols(0), weight_q)
-            return attn
-
-        def make_gain(h, wg_q):
-            gain_ps = bank((7, 2)[h], "gain_ps%d" % h)
-            for c in range(2):
-                product(gain_ps[:, Q * c : Q * (c + 1)], wg_q, cols(c), cond_q)
-            gain = sb.tile([P, 2 * Q], F32, name="gain%d" % h)
-            nc.scalar.copy(out=gain[:], in_=gain_ps[:])
-            return gain
-
-        def modulate(j, part, attn, gain):
-            nc.vector.scalar_tensor_tensor(
-                out=part,
-                in0=gain[:, Q * (j % 2) : Q * (j % 2 + 1)],
-                scalar=1.0,
-                in1=attn[:, 0:Q],
-                op0=ALU.add,
-                op1=ALU.mult,
+            probs[h] = prob_pair[:, h, :]
+            nc.scalar.activation(
+                out=probs[h], in_=scores[h][:], func=ACT.Exp, bias=neg_max[:], accum_out=row_sums[:, h : h + 1]
             )
 
-        def make_shift(j, wb_q, c):
-            shift = bank((3, 6, 2, 7)[j], "shift%d" % j)
-            product(shift[:, 0:Q], wb_q, cols(c), cond_q)
-            return shift
-
-        def finish(j, shift, part):
-            result = sb.tile([P, Q], F32, name="result%d" % j)
-            nc.vector.tensor_tensor(out=result[:], in0=shift[:, 0:Q], in1=part, op=ALU.add)
-            nc.sync.dma_start(out=out[cols(j), :], in_=result[:])
-
-        cond_q = quantise("cond", cond_bf)
-        val_bf = [gather_vals(0)]
-        wg_bf = weave(nc.scalar.copy, "wg0", wg_raw[0][:])
-
-        weight_bf = sb.tile([P, Q, PACK], BF16, name="weight_bf", align_bytes=64)
-        for h in range(2):
-            inv_sum = sb.tile([P, 1], F32, name="inv_sum%d" % h, tag=("val_pool0", "inv_sum1")[h], align_bytes=64)
-            nc.vector.reciprocal(out=inv_sum[:], in_=sums[h][:])
-            weight = sb.tile([P, I], BF16, name="weight%d" % h, align_bytes=64)
+        def weigh(h):
+            weight = held([P, I], BF16, "weight%d" % h, ("weight0", "weight1")[h])
             nc.vector.scalar_tensor_tensor(
                 out=weight[:].rearrange("q (s t) -> q s t", t=PACK),
-                in0=probs[h][:].rearrange("q (s t) -> q s t", t=PACK),
-                scalar=inv_sum[:],
+                in0=probs[h].rearrange("q (s t) -> q s t", t=PACK),
+                scalar=inv_sums[:, h : h + 1],
                 in1=size_rows[:].rearrange("q (t s) -> q s t", t=PACK),
                 op0=ALU.mult,
                 op1=ALU.mult,
@@ -209,35 +168,89 @@ def tile_attend_filmattn_kernel(tc, query, keys_words, keys_scales, size, vals, 
                 out=weight_bf[:, cols(h), :].bitcast(F32),
                 in_=weight_turned[:, 0:HALF].rearrange("p (u q) -> p q u", u=2),
             )
-        val_bf.append(gather_vals(1))
-        val_q = [quantise("val0", val_bf[0], slot="inv_sum1")]
-        gains = [make_gain(0, quantise("wg0", wg_bf, slot="prob1"))]
-        gains.append(make_gain(1, quantise("wg1", weave(nc.vector.tensor_copy, "wg1", wg_raw[1][:]))))
-        weight_q = quantise("weight", weight_bf, slot="wg1_bf")
-        val_q.append(quantise("val1", val_bf[1]))
-        attn = [attend(j, val_q[j]) for j in range(2)]
 
-        val_bf.append(gather_vals(2))
-        early = sb.tile([P, 2, Q], F32, name="early", tag="val_pool2", align_bytes=64)
-        parts = [early[:, 0, :], early[:, 1, :]]
-        for j in range(2):
-            modulate(j, parts[j], attn[j], gains[0])
-        val_bf.append(gather_vals(3))
-        attn.append(attend(2, quantise("val2", val_bf[2], slot="val_pool3")))
-        wb_bf = [
-            weave(nc.scalar.copy, "wb0", wb_raw[0][:]),
-            weave(nc.vector.tensor_copy, "wb2", wb_raw[1][:, :, cols(0)]),
-            weave(nc.scalar.copy, "wb3", wb_raw[1][:, :, cols(1)]),
-        ]
-        wb_q = [quantise("wb0", wb_bf[0])]
-        part2 = sb.tile([P, Q], F32, name="part2")
-        modulate(2, part2[:], attn[2], gains[1])
-        wb_q.append(quantise("wb2", wb_bf[1]))
-        attn.append(attend(3, quantise("val3", val_bf[3], slot="wb2_bf")))
-        for j in range(2):
-            finish(j, make_shift(j, wb_q[0], j), parts[j])
-        wb_q.append(quantise("wb3", wb_bf[2]))
-        finish(2, make_shift(2, wb_q[1], 0), part2[:])
-        part3 = sb.tile([P, Q], F32, name="part3", tag="val_pool2", align_bytes=64)
-        modulate(3, part3[:], attn[3], gains[1])
-        finish(3, make_shift(3, wb_q[2], 0), part3[:])
+        def gather_vals(j, woven):
+            picked = held([P, I], BF16, "picked%d" % j, ("picked0", "picked1", "picked2", "picked3")[j])
+            nc.vector.tensor_copy(picked[:], val_pool[j][:].indirect(offsets[:]))
+            turned = bank(4 + j % 2, "val_turned%d" % j)
+            turn(turned[:, 0:HALF], picked)
+            nc.scalar.copy(out=woven.bitcast(F32), in_=turned[:, 0:HALF].rearrange("p (u e) -> p e u", u=2))
+
+        def make_gain(h, wg_q, slot):
+            gain_ps = bank((7, 2)[h], "gain_ps%d" % h)
+            for c in range(2):
+                product(gain_ps[:, Q * c : Q * (c + 1)], wg_q, cols(c), cond_q)
+            nc.scalar.copy(out=gains[:, 2 * Q * h : 2 * Q * (h + 1)], in_=gain_ps[:])
+
+        def modulate(part, attn, gain):
+            nc.vector.scalar_tensor_tensor(out=part, in0=gain, scalar=1.0, in1=attn, op0=ALU.add, op1=ALU.mult)
+
+        def finish(first, count, shift, part, slot):
+            result = held([P, count * Q], F32, "result%d" % first, slot)
+            nc.vector.tensor_tensor(out=result[:], in0=shift, in1=part, op=ALU.add)
+            nc.sync.dma_start(
+                out=out[P * first : P * (first + count), :].rearrange("(c p) q -> p c q", p=P),
+                in_=result[:].rearrange("p (c q) -> p c q", q=Q),
+            )
+
+        weave(nc.scalar.copy, query_bf[0][:], query_raw[:, :, cols(0)])
+        weave(nc.scalar.copy, query_bf[1][:], query_raw[:, :, cols(1)])
+        score(0)
+        score(1)
+        first_bf = held([P, 2 * HALF, PACK], BF16, "first_bf")
+        weave(nc.scalar.copy, first_bf[:, 0:Q, :], cond_raw[:])
+        weave(nc.scalar.copy, first_bf[:, Q : Q + HALF, :], wg_raw[0][:])
+        soften(0)
+        soften(1)
+        first_q = quantise("first", first_bf, "first_codes")
+        cond_q = window(first_q, 0, Q)
+        gain0 = make_gain(0, window(first_q, Q, HALF), "gain0")
+        second_bf = held([P, P + Q, PACK], BF16, "second_bf", "wg1_raw")
+        val_bf0, weight_bf = second_bf[:, 0:P, :], second_bf[:, P : P + Q, :]
+        gather_vals(0, val_bf0[:])
+        wg_bf1 = held([P, HALF, PACK], BF16, "wg_bf1", "wg_bf1")
+        weave(nc.scalar.copy, wg_bf1[:], wg_raw[1][:])
+        val_q0 = quantise("val0", val_bf0, "val0_codes")
+        inv_sums = held([P, 2], F32, "inv_sums", "val_pool0")
+        nc.vector.reciprocal(out=inv_sums[:], in_=row_sums[:])
+        weigh(0)
+        weigh(1)
+        gain1 = make_gain(1, quantise("wg1", wg_bf1, "wg1_codes"), "gain1")
+        val_bf12 = held([P, 2 * P, PACK], BF16, "val_bf12", "val_bf12")
+        gather_vals(1, val_bf12[:, cols(0), :])
+        weight_q = quantise("weight", weight_bf, "val_pool1")
+        attn0 = bank(0, "attn0")
+        product(attn0[:, 0:Q], val_q0, cols(0), weight_q)
+        gather_vals(2, val_bf12[:, cols(1), :])
+        part0 = held([P, Q], F32, "part0", "val_pool2")
+        modulate(part0[:], attn0[:, 0:Q], gains[:, 0:Q])
+        val_bf3 = held([P, P, PACK], BF16, "val_bf3", "wb0_raw")
+        gather_vals(3, val_bf3[:])
+        val_q = quantise("val12", val_bf12, "val_pool3")
+        attn12 = bank(1, "attn12")
+        for c in range(2):
+            product(attn12[:, Q * c : Q * (c + 1)], val_q, cols(c), weight_q)
+        wb_bf0 = held([P, HALF, PACK], BF16, "wb_bf0", "wb_bf0")
+        weave(nc.scalar.copy, wb_bf0[:], wb_raw[0][:])
+        wb_q = quantise("wb0", wb_bf0, "wb0_codes")
+        shift01 = bank(3, "shift01")
+        for c in range(2):
+            product(shift01[:, Q * c : Q * (c + 1)], wb_q, cols(c), cond_q)
+        attn3 = bank(0, "attn3")
+        product(attn3[:, 0:Q], quantise("val3", val_bf3, "val3_codes"), cols(0), weight_q)
+        part12 = held([P, 2 * Q], F32, "part12", "wb_bf0")
+        modulate(part12[:], attn12[:], gains[:, Q : 3 * Q])
+        wb_bf2 = held([P, P, PACK], BF16, "wb_bf2", "wb_bf2")
+        weave(nc.scalar.copy, wb_bf2[:], wb_raw[1][:, :, cols(0)])
+        shift2 = bank(6, "shift2")
+        product(shift2[:, 0:Q], quantise("wb2", wb_bf2, "wb2_codes"), cols(0), cond_q)
+        wb_bf3 = held([P, P, PACK], BF16, "wb_bf3", "wb_bf3")
+        weave(nc.scalar.copy, wb_bf3[:], wb_raw[1][:, :, cols(1)])
+        finish(0, 1, shift01[:, 0:Q], part0[:], "result0")
+        finish(1, 1, shift01[:, Q : 2 * Q], part12[:, 0:Q], "result1")
+        shift3 = bank(7, "shift3")
+        product(shift3[:, 0:Q], quantise("wb3", wb_bf3, "wb3_codes"), cols(0), cond_q)
+        part3 = held([P, Q], F32, "part3", "part3")
+        modulate(part3[:], attn3[:, 0:Q], gains[:, 3 * Q : 4 * Q])
+        finish(2, 1, shift2[:, 0:Q], part12[:, Q : 2 * Q], "result2")
+        finish(3, 1, shift3[:, 0:Q], part3[:], "result3")

from contextlib import ExitStack

import concourse.mybir as mybir
from concourse.masks import make_identity

D, T, I, Q, E, K = 512, 2048, 512, 256, 512, 512
FLOPS = 2 * Q * I * D + 2 * E * Q * I + 2 * 2 * E * Q * K

F32 = mybir.dt.float32
BF16 = mybir.dt.bfloat16
I32 = mybir.dt.int32
U32 = mybir.dt.uint32
U16 = mybir.dt.uint16
U8 = mybir.dt.uint8
FP8X4 = mybir.dt.float8_e4m3fn_x4
FP4X4 = mybir.dt.float4_e2m1fn_x4
ALU = mybir.AluOpType
ACT = mybir.ActivationFunctionType
AX = mybir.AxisListType

P = 128
PACK = 4
HALF = 256


def tile_attend_filmattn_kernel(tc, query, keys_words, keys_scales, size, vals, cond, wg, wb, offs, out):
    nc = tc.nc
    with ExitStack() as ctx:
        sb = ctx.enter_context(tc.tile_pool(name="sb", bufs=1))
        ps = ctx.enter_context(tc.psum_pool(name="ps", bufs=1))

        def bank(n, name):
            return ps.tile([P, 512], F32, tag="bank%d" % n, name=name)

        def held(shape, dtype, name, slot=None):
            return sb.tile(shape, dtype, name=name, tag=slot or name, align_bytes=64)

        def load_rows(name, src):
            raw = held([P, PACK, HALF], F32, name + "_raw")
            nc.sync.dma_start(out=raw[:], in_=src)
            return raw

        def weave(copy, woven, raw):
            copy(
                out=woven.rearrange("p (c i) t -> p c t i", i=4),
                in_=raw.rearrange("p t (c i) -> p c t i", i=4),
            )

        def quantise(name, woven, slot=None):
            width = woven.shape[1]
            codes = held([P, width], U32, name + "_codes", slot)
            scales = held([P, width], U8, name + "_scales")
            nc.vector.quantize_mx(
                out=codes[:].bitcast(FP8X4), scales=scales[:], in_=woven[:].rearrange("p c t -> p (c t)")
            )
            return codes[:], scales[:]

        def window(quantised, first, width):
            return quantised[0][:, first : first + width], quantised[1][:, first : first + width]

        def product(dst, stat, cols, mov):
            nc.tensor.matmul_mx(
                out=dst,
                lhsT=stat[0][:, cols].bitcast(FP8X4),
                lhsT_scale=stat[1][:, cols],
                rhs=mov[0].bitcast(FP8X4),
                rhs_scale=mov[1],
                start=True,
                stop=True,
            )

        def turn(dst, src_bf):
            words = src_bf[:].bitcast(F32)
            for u in range(2):
                nc.tensor.transpose(dst[:, P * u : P * (u + 1)], words[:, u : 2 * P : 2], ident[:])

        def load_vals(j):
            pool_j = sb.tile([P, T], F32, name="val_pool%d" % j, tag="val_pool%d" % j, align_bytes=64)
            nc.sync.dma_start(out=pool_j[:], in_=vals[P * j : P * (j + 1), :])
            return pool_j

        def rows4(ap):
            return ap.rearrange("(p j) c -> p j c", j=PACK)

        def load_half(name, w, h):
            return load_rows("%s%d" % (name, h), rows4(w)[:, :, HALF * h : HALF * (h + 1)])

        def cols(c):
            return slice(P * c, P * (c + 1))

        scale_pool = held([P, T], U8, "scale_pool")
        nc.gpsimd.memset(scale_pool[:].bitcast(I32), 0)
        offsets = sb.tile([P, I // 16], U16, name="offsets")
        nc.sync.dma_start(offsets[:], offs)
        val_pool, wg_raw, wb_raw = {}, {}, {}
        size_col = sb.tile([P, PACK], F32, name="size_col")
        nc.sync.dma_start(out=size_col[:], in_=size.rearrange("o (p t) -> p (o t)", t=PACK))
        key_pool = held([P, T], U16, "key_pool")
        nc.sync.dma_start(out=key_pool[:].bitcast(I32), in_=keys_words[0].bitcast(I32))
        for quad in range(4):
            nc.sync.dma_start(
                out=scale_pool[32 * quad : 32 * quad + 4, :].bitcast(I32),
                in_=keys_scales[0, 4 * quad : 4 * quad + 4, :].bitcast(I32),
            )
        query_raw = load_rows("query", rows4(query))
        cond_raw = load_rows("cond", rows4(cond))
        wg_raw[0] = load_half("wg", wg, 0)
        val_pool[0] = load_vals(0)
        wg_raw[1] = load_half("wg", wg, 1)
        val_pool[1] = load_vals(1)
        val_pool[2] = load_vals(2)
        val_pool[3] = load_vals(3)
        wb_raw[0] = load_half("wb", wb, 0)
        wb_raw[1] = load_half("wb", wb, 1)

        ident = sb.tile([P, P], F32, name="ident")
        make_identity(nc, ident[:])

        key_codes = held([P, I], U16, "key_codes")
        nc.vector.tensor_copy(key_codes[:], key_pool[:].indirect(offsets[:]))
        key_scales = held([P, I], U8, "key_scales")
        nc.vector.tensor_copy(key_scales[:], scale_pool[:].indirect(offsets[:]))

        size_rows = bank(2, "size_rows")
        for t in range(PACK):
            nc.tensor.transpose(size_rows[:, cols(t)], size_col[:, t : t + 1].to_broadcast([P, P]), ident[:])

        query_bf = [held([P, P, PACK], BF16, "query_bf%d" % h) for h in range(2)]
        gains = held([P, 4 * Q], F32, "gains")
        scores, probs = {}, {}
        prob_pair = held([P, 2, I], F32, "prob_pair", "wg0_raw")
        row_sums = held([P, 2], F32, "row_sums")

        def score(h):
            query_q = quantise("query%d" % h, query_bf[h])
            scores[h] = bank(h, "score%d" % h)
            nc.tensor.matmul_mx(
                out=scores[h][:],
                lhsT=query_q[0].bitcast(FP8X4),
                lhsT_scale=query_q[1],
                rhs=key_codes[:].bitcast(FP4X4),
                rhs_scale=key_scales[:],
                start=True,
                stop=True,
            )

        def soften(h):
            neg_max = held([P, 1], F32, "neg_max%d" % h, ("neg_max0", "neg_max1")[h])
            nc.vector.tensor_reduce(out=neg_max[:], in_=scores[h][:], axis=AX.X, op=ALU.max, negate=True)
            probs[h] = prob_pair[:, h, :]
            nc.scalar.activation(
                out=probs[h], in_=scores[h][:], func=ACT.Exp, bias=neg_max[:], accum_out=row_sums[:, h : h + 1]
            )

        def weigh(h):
            weight = held([P, I], BF16, "weight%d" % h, ("weight0", "weight1")[h])
            nc.vector.scalar_tensor_tensor(
                out=weight[:].rearrange("q (s t) -> q s t", t=PACK),
                in0=probs[h].rearrange("q (s t) -> q s t", t=PACK),
                scalar=inv_sums[:, h : h + 1],
                in1=size_rows[:].rearrange("q (t s) -> q s t", t=PACK),
                op0=ALU.mult,
                op1=ALU.mult,
            )
            weight_turned = bank((3, 6)[h], "weight_turned%d" % h)
            turn(weight_turned[:, 0:HALF], weight)
            nc.scalar.copy(
                out=weight_bf[:, cols(h), :].bitcast(F32),
                in_=weight_turned[:, 0:HALF].rearrange("p (u q) -> p q u", u=2),
            )

        def gather_vals(j, woven):
            picked = held([P, I], BF16, "picked%d" % j, ("picked0", "picked1", "picked2", "picked3")[j])
            nc.vector.tensor_copy(picked[:], val_pool[j][:].indirect(offsets[:]))
            turned = bank(4 + j % 2, "val_turned%d" % j)
            turn(turned[:, 0:HALF], picked)
            nc.scalar.copy(out=woven.bitcast(F32), in_=turned[:, 0:HALF].rearrange("p (u e) -> p e u", u=2))

        def make_gain(h, wg_q, slot):
            gain_ps = bank((7, 2)[h], "gain_ps%d" % h)
            for c in range(2):
                product(gain_ps[:, Q * c : Q * (c + 1)], wg_q, cols(c), cond_q)
            nc.scalar.copy(out=gains[:, 2 * Q * h : 2 * Q * (h + 1)], in_=gain_ps[:])

        def modulate(part, attn, gain):
            nc.vector.scalar_tensor_tensor(out=part, in0=gain, scalar=1.0, in1=attn, op0=ALU.add, op1=ALU.mult)

        def finish(first, count, shift, part, slot):
            result = held([P, count * Q], F32, "result%d" % first, slot)
            nc.vector.tensor_tensor(out=result[:], in0=shift, in1=part, op=ALU.add)
            nc.sync.dma_start(
                out=out[P * first : P * (first + count), :].rearrange("(c p) q -> p c q", p=P),
                in_=result[:].rearrange("p (c q) -> p c q", q=Q),
            )

        weave(nc.scalar.copy, query_bf[0][:], query_raw[:, :, cols(0)])
        weave(nc.scalar.copy, query_bf[1][:], query_raw[:, :, cols(1)])
        score(0)
        score(1)
        first_bf = held([P, 2 * HALF, PACK], BF16, "first_bf")
        weave(nc.scalar.copy, first_bf[:, 0:Q, :], cond_raw[:])
        weave(nc.scalar.copy, first_bf[:, Q : Q + HALF, :], wg_raw[0][:])
        soften(0)
        soften(1)
        first_q = quantise("first", first_bf, "first_codes")
        cond_q = window(first_q, 0, Q)
        gain0 = make_gain(0, window(first_q, Q, HALF), "gain0")
        second_bf = held([P, P + Q, PACK], BF16, "second_bf", "wg1_raw")
        val_bf0, weight_bf = second_bf[:, 0:P, :], second_bf[:, P : P + Q, :]
        gather_vals(0, val_bf0[:])
        wg_bf1 = held([P, HALF, PACK], BF16, "wg_bf1", "wg_bf1")
        weave(nc.scalar.copy, wg_bf1[:], wg_raw[1][:])
        val_q0 = quantise("val0", val_bf0, "val0_codes")
        inv_sums = held([P, 2], F32, "inv_sums", "val_pool0")
        nc.vector.reciprocal(out=inv_sums[:], in_=row_sums[:])
        weigh(0)
        weigh(1)
        gain1 = make_gain(1, quantise("wg1", wg_bf1, "wg1_codes"), "gain1")
        val_bf12 = held([P, 2 * P, PACK], BF16, "val_bf12", "val_bf12")
        gather_vals(1, val_bf12[:, cols(0), :])
        weight_q = quantise("weight", weight_bf, "val_pool1")
        attn0 = bank(0, "attn0")
        product(attn0[:, 0:Q], val_q0, cols(0), weight_q)
        gather_vals(2, val_bf12[:, cols(1), :])
        part0 = held([P, Q], F32, "part0", "val_pool2")
        modulate(part0[:], attn0[:, 0:Q], gains[:, 0:Q])
        val_bf3 = held([P, P, PACK], BF16, "val_bf3", "wb0_raw")
        gather_vals(3, val_bf3[:])
        val_q = quantise("val12", val_bf12, "val_pool3")
        attn12 = bank(1, "attn12")
        for c in range(2):
            product(attn12[:, Q * c : Q * (c + 1)], val_q, cols(c), weight_q)
        wb_bf0 = held([P, HALF, PACK], BF16, "wb_bf0", "wb_bf0")
        weave(nc.scalar.copy, wb_bf0[:], wb_raw[0][:])
        wb_q = quantise("wb0", wb_bf0, "wb0_codes")
        shift01 = bank(3, "shift01")
        for c in range(2):
            product(shift01[:, Q * c : Q * (c + 1)], wb_q, cols(c), cond_q)
        attn3 = bank(0, "attn3")
        product(attn3[:, 0:Q], quantise("val3", val_bf3, "val3_codes"), cols(0), weight_q)
        part12 = held([P, 2 * Q], F32, "part12", "wb_bf0")
        modulate(part12[:], attn12[:], gains[:, Q : 3 * Q])
        wb_bf2 = held([P, P, PACK], BF16, "wb_bf2", "wb_bf2")
        weave(nc.scalar.copy, wb_bf2[:], wb_raw[1][:, :, cols(0)])
        shift2 = bank(6, "shift2")
        product(shift2[:, 0:Q], quantise("wb2", wb_bf2, "wb2_codes"), cols(0), cond_q)
        wb_bf3 = held([P, P, PACK], BF16, "wb_bf3", "wb_bf3")
        weave(nc.scalar.copy, wb_bf3[:], wb_raw[1][:, :, cols(1)])
        finish(0, 1, shift01[:, 0:Q], part0[:], "result0")
        finish(1, 1, shift01[:, Q : 2 * Q], part12[:, 0:Q], "result1")
        shift3 = bank(7, "shift3")
        product(shift3[:, 0:Q], quantise("wb3", wb_bf3, "wb3_codes"), cols(0), cond_q)
        part3 = held([P, Q], F32, "part3", "part3")
        modulate(part3[:], attn3[:, 0:Q], gains[:, 3 * Q : 4 * Q])
        finish(2, 1, shift2[:, 0:Q], part12[:, Q : 2 * Q], "result2")
        finish(3, 1, shift3[:, 0:Q], part3[:], "result3")
